import numpy as np
import ml_dtypes


def mxq(x, axis, fmt="e4m3"):
    dtype, down = {"e4m3": (ml_dtypes.float8_e4m3fn, 7), "e5m2": (ml_dtypes.float8_e5m2, 14)}[fmt]
    v = np.moveaxis(np.asarray(x, np.float32).astype(ml_dtypes.bfloat16).astype(np.float64), axis, -1)
    blocks = v.reshape(v.shape[:-1] + (-1, 32))
    amax = np.abs(blocks).max(-1, keepdims=True)
    byte = np.maximum(np.where(amax > 0, np.frexp(amax)[1] - 1 + 127, 0) - down, 1)
    scale = np.exp2(byte - 127.0)
    codes = (blocks / scale).astype(np.float32).astype(dtype).astype(np.float64)
    return np.moveaxis((codes * scale).reshape(v.shape), -1, axis)


WIDE = False


def mx_kscale(k):
    if not WIDE:
        return np.ones(k)
    levels = np.array([10, -10, 5, -5, 0])
    if k % 512:
        return np.exp2(np.random.permutation(np.resize(levels, k // 32))).repeat(32)
    a = np.empty((k // 512, 16))
    for p in range(k // 512):
        a[p, :8] = np.random.permutation(np.resize(levels, 8))
        for g in range(8):
            far = levels[np.abs(levels - a[p, g]) >= 10]
            a[p, g + 8] = far[np.random.randint(len(far))]
    return np.exp2(a.ravel()).repeat(32)


def f64(x):
    return np.asarray(x).astype(np.float64)


def striped(idx):
    return np.tile(idx.reshape(-1, 16).T, (8, 1)).astype(np.uint16)


def unstriped(offs):
    return offs[:16].T.reshape(-1).astype(np.int64)


def pack_weight(w):
    k, n = w.shape
    w = f64(np.asarray(w, np.float32).astype(ml_dtypes.bfloat16)).reshape(k // 32, 32, n)
    amax = np.abs(w).max(1)
    byte = np.clip(np.where(amax > 0, np.frexp(amax)[1] - 1 + 127 - 7, 1), 1, 254)
    scaled = (w * np.exp2(127.0 - byte)[:, None, :]).reshape(k, n).astype(np.float32)
    words = np.ascontiguousarray(scaled.reshape(k // 512, 128, 4, n).transpose(0, 1, 3, 2)).astype(ml_dtypes.float8_e4m3fn).view(np.uint8)
    return words, np.ascontiguousarray(byte.astype(np.uint8).reshape(k // 512, 16, n))


def unpack_weight(words, scales):
    g, p, n, _ = words.shape
    vals = np.ascontiguousarray(words).view(ml_dtypes.float8_e4m3fn).astype(np.float64) * np.repeat(np.exp2(scales.astype(np.float64) - 127.0), 8, axis=1)[..., None]
    return vals.transpose(0, 1, 3, 2).reshape(g * 512, n)


def sigmoid(v):
    return 1.0 / (1.0 + np.exp(-np.maximum(v, -700.0)))


K, T, S, H, J, N, U = 512, 1024, 512, 512, 512, 512, 1024
P = 2 ** 7


def setup_inputs():
    n = np.random.standard_normal
    s = mx_kscale(K)[:, None]
    u = mx_kscale(H)
    packed_xT = pack_weight(n((K, T)) * s)
    return {
        "x_words": packed_xT[0],
        "x_scales": packed_xT[1],
        "mem": (n((H, U)) * u[:, None]).astype(np.float32),
        "wd": (n((H, J)) / np.sqrt(H) / u[:, None]).astype(np.float32),
        "w1": (n((K, N)) / np.sqrt(K) / s).astype(np.float32),
        "w2": (n((K, N)) / np.sqrt(K) / s).astype(np.float32),
        "w3": (n((K, N)) / np.sqrt(K) / s).astype(np.float32),
        "unit": (np.random.uniform(0.6, 1.4, (H, 1)) / u[:, None]).astype(np.float32),
        "fade": (np.tile(np.random.uniform(0.1, 1.0, S), (P, 1))).astype(np.float32),
        "offs": striped(np.random.permutation(T)[:S]),
        "slot": striped(np.random.permutation(U)[:S]),
    }


def reference(x_words, x_scales, mem, wd, w1, w2, w3, unit, fade, offs, slot):
    xq = unpack_weight(x_words, x_scales)[:, unstriped(offs)]
    f = sigmoid(mxq(f64(w1), 0, "e4m3").T @ xq)
    old = f64(mem)[:, unstriped(slot)]
    ov = f64(unit) * old
    cs = np.tanh(mxq(f64(wd), 0, "e4m3").T @ mxq(old, 0, "e4m3"))
    adj = ov - cs + cs * f64(fade)[:1]
    a = sigmoid(mxq(f64(w2), 0, "e4m3").T @ xq)
    return f * adj + a * (np.tanh(mxq(f64(w3), 0, "e4m3").T @ xq))

@@ -1,0 +1,315 @@
+from contextlib import ExitStack
+
+import concourse.mybir as mybir
+from concourse.masks import make_identity
+
+F32 = mybir.dt.float32
+BF16 = mybir.dt.bfloat16
+I32 = mybir.dt.int32
+U32 = mybir.dt.uint32
+U16 = mybir.dt.uint16
+U8 = mybir.dt.uint8
+FP8X4 = mybir.dt.float8_e4m3fn_x4
+ACT = mybir.ActivationFunctionType
+ALU = mybir.AluOpType
+
+P = 128
+PACK = 4
+VISITS = 1024
+PICKED = 512
+UNITS = 512
+HALF = 256
+FLOPS = 4 * 2 * 512 * 512 * 512
+
+
+def tile_picked_ytlstm_cell_p_kernel(
+    tc, x_words, x_scales, mem, wd, w1, w2, w3, unit, fade, offs, slot, out
+):
+    nc = tc.nc
+    with ExitStack() as ctx:
+        keep = ctx.enter_context(tc.tile_pool(name="keep", bufs=1))
+        psum = ctx.enter_context(tc.psum_pool(name="psum", bufs=1))
+
+        def bank_tile(b, shape):
+            return psum.tile(shape, F32, name="bank", tag="bank%d" % b)
+
+        def sb(name, shape, dtype):
+            return keep.tile(shape, dtype, name=name, align_bytes=64)
+
+        offs_t = keep.tile([P, PICKED // 16], U16, name="offs_t")
+        slot_t = keep.tile([P, PICKED // 16], U16, name="slot_t")
+        xw_all = sb("xw_all", [P, VISITS], U32)
+        xs_all = sb("xs_all", [P, VISITS], U8)
+        fade_rows = sb("fade_rows", [P, P], F32)
+        ident = sb("ident", [P, P], F32)
+        unit_t = sb("unit_t", [P, PACK], F32)
+        mem_t = [sb("mem_%d" % t, [P, VISITS], F32) for t in range(PACK)]
+        weights = {"w1": w1, "w2": w2, "w3": w3, "wd": wd}
+        w_raw = {(n, h): sb("raw_%s_%d" % (n, h), [P, PACK, HALF], F32) for n in weights for h in range(2)}
+
+        nc.vector.memset(xs_all[:].bitcast(I32), 0)
+        nc.gpsimd.memset(fade_rows[:], 0.0)
+        make_identity(nc, ident[:])
+        warm = sb("warm", [P, 2], F32)
+        nc.vector.memset(warm[:, 0:1], 0.0)
+        nc.scalar.activation(out=warm[:, 1:2], in_=warm[:, 0:1], func=ACT.Sigmoid)
+
+        def load_w(n, h):
+            src = weights[n].rearrange("(p t) n -> p t n", t=PACK)
+            nc.sync.dma_start(out=w_raw[n, h][:], in_=src[:, :, h * HALF : (h + 1) * HALF])
+
+        def load_mem(t):
+            nc.sync.dma_start(out=mem_t[t][:], in_=mem.rearrange("(p t) c -> t p c", t=PACK)[t])
+
+        def load_x():
+            nc.sync.dma_start(out=xw_all[:].bitcast(I32), in_=x_words[0].rearrange("p n t -> p (n t)").bitcast(I32))
+
+        def load_xs(q):
+            nc.sync.dma_start(
+                out=xs_all[32 * q : 32 * q + 4, :].bitcast(I32), in_=x_scales[0, 4 * q : 4 * q + 4, :].bitcast(I32)
+            )
+
+        def load_unit():
+            nc.sync.dma_start(out=unit_t[:], in_=unit.rearrange("(p t) o -> p (t o)", t=PACK))
+
+        def load_fade():
+            nc.sync.dma_start(out=fade_rows[0:4, :], in_=fade[0:1, :].rearrange("o (c j) -> (o c) j", c=4))
+
+        nc.sync.dma_start(offs_t[:], offs)
+        load_xs(0)
+        load_xs(1)
+        load_xs(2)
+        load_xs(3)
+        load_x()
+        load_w("w2", 0)
+        nc.sync.dma_start(slot_t[:], slot)
+        load_w("w3", 0)
+        load_unit()
+        load_mem(0)
+        load_fade()
+        load_w("w2", 1)
+        load_mem(1)
+        load_mem(2)
+        load_w("w3", 1)
+        load_mem(3)
+        load_w("wd", 0)
+        load_w("wd", 1)
+        load_w("w1", 0)
+        load_w("w1", 1)
+
+        xw = sb("xw", [P, PICKED], U32)
+        xs = sb("xs", [P, PICKED], U8)
+        old = sb("old", [P, PACK, PICKED], F32)
+        ov = sb("ov", [P, PACK, PICKED], F32)
+        fm1 = sb("fm1", [P, 4], F32)
+        grouped = {}
+        codes = {n: sb("codes_" + n, [P, 512], U32) for n in ("w1", "w2", "w3", "wd", "old")}
+        scales = {n: sb("scales_" + n, [P, 512], U8) for n in ("w1", "w2", "w3", "wd", "old")}
+        gate = {n: sb("gate_" + n, [P, 4, UNITS], F32) for n in ("w1", "w2", "w3", "wd")}
+        adj = sb("adj", [P, 4, UNITS], F32)
+        kept = sb("kept", [P, 4, UNITS], F32)
+        fresh = sb("fresh", [P, 4, UNITS], F32)
+
+        def cast(n, h, on_scalar):
+            src = old[:, :, h * HALF : (h + 1) * HALF] if n == "old" else w_raw[n, h][:]
+            dst = sb("grouped_%s_%d" % (n, h), [P, HALF, PACK], BF16)
+            grouped[n, h] = dst
+            o = dst[:].rearrange("p (c i) t -> p c t i", i=4)
+            s = src.rearrange("p t (c i) -> p c t i", i=4)
+            if on_scalar:
+                nc.scalar.copy(out=o, in_=s)
+            else:
+                nc.vector.tensor_copy(out=o, in_=s)
+
+        def quantise(n, h):
+            cols = slice(h * HALF, (h + 1) * HALF)
+            nc.vector.quantize_mx(
+                out=codes[n][:, cols].bitcast(FP8X4),
+                scales=scales[n][:, cols],
+                in_=grouped[n, h][:].rearrange("p c t -> p (c t)"),
+            )
+
+        def gate_unit(n, h, u, func, b):
+            bank = bank_tile(b, [P, 2, HALF])
+            cols = slice(h * HALF, (h + 1) * HALF)
+            for k in range(2):
+                js = slice((2 * u + k) * P, (2 * u + k + 1) * P)
+                nc.tensor.matmul_mx(
+                    out=bank[:, k, :],
+                    lhsT=xw[:, js].bitcast(FP8X4),
+                    lhsT_scale=xs[:, js],
+                    rhs=codes[n][:, cols].bitcast(FP8X4),
+                    rhs_scale=scales[n][:, cols],
+                    start=True,
+                    stop=True,
+                )
+            nc.scalar.activation(out=gate[n][:, 2 * u : 2 * u + 2, cols], in_=bank[:], func=func)
+
+        def gather_words():
+            nc.vector.tensor_copy(out=xw[:], in_=xw_all[:].indirect(offs_t[:]))
+
+        def gather_scales():
+            nc.vector.tensor_copy(out=xs[:], in_=xs_all[:].indirect(offs_t[:]))
+
+        def gather_mem(t):
+            nc.vector.tensor_copy(out=old[:, t, :], in_=mem_t[t][:].indirect(slot_t[:]))
+
+        def scale_old(t, engine="S"):
+            if engine == "S":
+                nc.scalar.activation(out=ov[:, t, :], in_=old[:, t, :], func=ACT.Copy, scale=unit_t[:, t : t + 1])
+            elif engine == "V":
+                nc.vector.tensor_scalar(
+                    out=ov[:, t, :], in0=old[:, t, :], scalar1=unit_t[:, t : t + 1], scalar2=None, op0=ALU.mult
+                )
+            else:
+                nc.gpsimd.tensor_scalar(
+                    out=ov[:, t, :], in0=old[:, t, :], scalar1=unit_t[:, t : t + 1], scalar2=0.0, op0=ALU.mult, op1=ALU.add
+                )
+
+        def fade_prep(b):
+            fade_bank = bank_tile(b, [P, P])
+            nc.tensor.transpose(fade_bank[:], fade_rows[:], ident[:])
+            nc.scalar.activation(out=fm1[:], in_=fade_bank[:, 0:4], func=ACT.Copy, bias=-1.0)
+
+        def fresh_unit(h, u):
+            w = (slice(None), slice(2 * u, 2 * u + 2), slice(h * HALF, (h + 1) * HALF))
+            nc.vector.tensor_tensor(out=fresh[w], in0=gate["w2"][w], in1=gate["w3"][w], op=ALU.mult)
+
+        def kept_unit(h, u):
+            w = (slice(None), slice(2 * u, 2 * u + 2), slice(h * HALF, (h + 1) * HALF))
+            nc.vector.tensor_tensor(out=kept[w], in0=gate["w1"][w], in1=adj[w], op=ALU.mult)
+
+        def short_term(jt, b):
+            js = slice(jt * P, (jt + 1) * P)
+            bank = bank_tile(b, [P, UNITS])
+            nc.tensor.matmul_mx(
+                out=bank[:],
+                lhsT=codes["old"][:, js].bitcast(FP8X4),
+                lhsT_scale=scales["old"][:, js],
+                rhs=codes["wd"][:].bitcast(FP8X4),
+                rhs_scale=scales["wd"][:],
+                start=True,
+                stop=True,
+            )
+            nc.scalar.activation(out=gate["wd"][:, jt, :], in_=bank[:], func=ACT.Tanh)
+
+        turned_ov = {}
+
+        def turn_ov(jt, b):
+            js = slice(jt * P, (jt + 1) * P)
+            turned = bank_tile(b, [P, PACK, P])
+            turned_ov[jt] = turned
+            for t in range(PACK):
+                nc.tensor.transpose(turned[:, t, :], ov[:, t, js], ident[:])
+
+        def adjust(jt):
+            turned = turned_ov[jt]
+            nc.vector.scalar_tensor_tensor(
+                out=adj[:, jt, :].rearrange("j (p t) -> j p t", t=PACK),
+                in0=gate["wd"][:, jt, :].rearrange("j (p t) -> j p t", t=PACK),
+                scalar=fm1[:, jt : jt + 1],
+                in1=turned[:].rearrange("j t p -> j p t"),
+                op0=ALU.mult,
+                op1=ALU.add,
+            )
+
+        totals = {}
+
+        def turn(src, h, u, first):
+            if first:
+                totals[h, u] = bank_tile(4 + 2 * h + u, [P, 2, HALF])
+            total = totals[h, u]
+            for b in range(2):
+                for k in range(2):
+                    i0 = h * HALF + b * P
+                    nc.tensor.matmul(
+                        total[:, b, k * P : (k + 1) * P],
+                        src[:, 2 * u + k, i0 : i0 + P],
+                        ident[:],
+                        start=(first and b == 0 and k == 0),
+                        stop=(not first and b == 1 and k == 1),
+                        is_transpose=True,
+                    )
+
+        def finish(h, u, on_scalar):
+            turn(kept, h, u, False)
+            total = totals[h, u]
+            res = sb("res_%d_%d" % (h, u), [P, 2, HALF], F32)
+            if on_scalar:
+                nc.scalar.copy(out=res[:], in_=total[:])
+            else:
+                nc.vector.tensor_copy(out=res[:], in_=total[:])
+            dst = out[h * HALF : (h + 1) * HALF, u * HALF : (u + 1) * HALF].rearrange("(b i) j -> i b j", b=2)
+            nc.sync.dma_start(out=dst, in_=res[:])
+
+        gather_scales()
+        gather_words()
+        cast("w2", 0, True)
+        fade_prep(7)
+        quantise("w2", 0)
+        cast("w3", 0, True)
+        gate_unit("w2", 0, 0, ACT.Sigmoid, 0)
+        gate_unit("w2", 0, 1, ACT.Sigmoid, 1)
+        gather_mem(0)
+        quantise("w3", 0)
+        cast("w2", 1, False)
+        gate_unit("w3", 0, 0, ACT.Tanh, 2)
+        gate_unit("w3", 0, 1, ACT.Tanh, 3)
+        quantise("w2", 1)
+        gather_mem(1)
+        scale_old(0)
+        gate_unit("w2", 1, 0, ACT.Sigmoid, 0)
+        gate_unit("w2", 1, 1, ACT.Sigmoid, 1)
+        gather_mem(2)
+        scale_old(1)
+        fresh_unit(0, 0)
+        cast("w3", 1, True)
+        gather_mem(3)
+        turn(fresh, 0, 0, True)
+        scale_old(2)
+        quantise("w3", 1)
+        scale_old(3)
+        cast("old", 0, False)
+        gate_unit("w3", 1, 0, ACT.Tanh, 0)
+        gate_unit("w3", 1, 1, ACT.Tanh, 1)
+        turn_ov(0, 2)
+        turn_ov(1, 3)
+        cast("wd", 0, False)
+        quantise("old", 0)
+        cast("wd", 1, True)
+        quantise("wd", 0)
+        cast("old", 1, False)
+        turn_ov(2, 6)
+        turn_ov(3, 7)
+        fresh_unit(0, 1)
+        quantise("wd", 1)
+        cast("w1", 0, True)
+        quantise("old", 1)
+        short_term(0, 0)
+        short_term(1, 1)
+        cast("w1", 1, False)
+        turn(fresh, 0, 1, True)
+        quantise("w1", 0)
+        short_term(2, 0)
+        short_term(3, 1)
+        fresh_unit(1, 0)
+        quantise("w1", 1)
+        adjust(0)
+        adjust(1)
+        gate_unit("w1", 0, 0, ACT.Sigmoid, 2)
+        gate_unit("w1", 1, 0, ACT.Sigmoid, 3)
+        fresh_unit(1, 1)
+        adjust(2)
+        adjust(3)
+        gate_unit("w1", 0, 1, ACT.Sigmoid, 0)
+        gate_unit("w1", 1, 1, ACT.Sigmoid, 1)
+        turn(fresh, 1, 0, True)
+        kept_unit(0, 0)
+        kept_unit(1, 0)
+        turn(fresh, 1, 1, True)
+        kept_unit(0, 1)
+        finish(0, 0, True)
+        kept_unit(1, 1)
+        finish(1, 0, True)
+        finish(0, 1, False)
+        finish(1, 1, True)

@@ -45,18 +45,17 @@ def tile_picked_ytlstm_cell_p_kernel(
         unit_t = sb("unit_t", [P, PACK], F32)
         mem_t = [sb("mem_%d" % t, [P, VISITS], F32) for t in range(PACK)]
         weights = {"w1": w1, "w2": w2, "w3": w3, "wd": wd}
-        w_raw = {(n, h): sb("raw_%s_%d" % (n, h), [P, PACK, HALF], F32) for n in weights for h in range(2)}
+        w_raw = {n: sb("raw_" + n, [P, PACK, UNITS], F32) for n in weights}
 
-        nc.vector.memset(xs_all[:].bitcast(I32), 0)
+        nc.gpsimd.memset(xs_all[:].bitcast(I32), 0)
+        warm = sb("warm", [P, 2], F32)
+        nc.gpsimd.memset(warm[:, 0:1], 0.0)
+        nc.scalar.activation(out=warm[:, 1:2], in_=warm[:, 0:1], func=ACT.Sigmoid)
         nc.gpsimd.memset(fade_rows[:], 0.0)
         make_identity(nc, ident[:])
-        warm = sb("warm", [P, 2], F32)
-        nc.vector.memset(warm[:, 0:1], 0.0)
-        nc.scalar.activation(out=warm[:, 1:2], in_=warm[:, 0:1], func=ACT.Sigmoid)
 
-        def load_w(n, h):
-            src = weights[n].rearrange("(p t) n -> p t n", t=PACK)
-            nc.sync.dma_start(out=w_raw[n, h][:], in_=src[:, :, h * HALF : (h + 1) * HALF])
+        def load_w(n):
+            nc.sync.dma_start(out=w_raw[n][:], in_=weights[n].rearrange("(p t) n -> p t n", t=PACK))
 
         def load_mem(t):
             nc.sync.dma_start(out=mem_t[t][:], in_=mem.rearrange("(p t) c -> t p c", t=PACK)[t])
@@ -75,27 +74,23 @@ def tile_picked_ytlstm_cell_p_kernel(
         def load_fade():
             nc.sync.dma_start(out=fade_rows[0:4, :], in_=fade[0:1, :].rearrange("o (c j) -> (o c) j", c=4))
 
+        load_x()
         nc.sync.dma_start(offs_t[:], offs)
         load_xs(0)
         load_xs(1)
         load_xs(2)
         load_xs(3)
-        load_x()
-        load_w("w2", 0)
+        load_w("w2")
         nc.sync.dma_start(slot_t[:], slot)
-        load_w("w3", 0)
-        load_unit()
         load_mem(0)
+        load_unit()
         load_fade()
-        load_w("w2", 1)
         load_mem(1)
         load_mem(2)
-        load_w("w3", 1)
+        load_w("w3")
         load_mem(3)
-        load_w("wd", 0)
-        load_w("wd", 1)
-        load_w("w1", 0)
-        load_w("w1", 1)
+        load_w("wd")
+        load_w("w1")
 
         xw = sb("xw", [P, PICKED], U32)
         xs = sb("xs", [P, PICKED], U8)
@@ -111,7 +106,7 @@ def tile_picked_ytlstm_cell_p_kernel(
         fresh = sb("fresh", [P, 4, UNITS], F32)
 
         def cast(n, h, on_scalar):
-            src = old[:, :, h * HALF : (h + 1) * HALF] if n == "old" else w_raw[n, h][:]
+            src = (old if n == "old" else w_raw[n])[:, :, h * HALF : (h + 1) * HALF]
             dst = sb("grouped_%s_%d" % (n, h), [P, HALF, PACK], BF16)
             grouped[n, h] = dst
             o = dst[:].rearrange("p (c i) t -> p c t i", i=4)
@@ -144,6 +139,20 @@ def tile_picked_ytlstm_cell_p_kernel(
                     stop=True,
                 )
             nc.scalar.activation(out=gate[n][:, 2 * u : 2 * u + 2, cols], in_=bank[:], func=func)
+
+        def gate_row(n, jt, func, b):
+            bank = bank_tile(b, [P, UNITS])
+            js = slice(jt * P, (jt + 1) * P)
+            nc.tensor.matmul_mx(
+                out=bank[:],
+                lhsT=xw[:, js].bitcast(FP8X4),
+                lhsT_scale=xs[:, js],
+                rhs=codes[n][:].bitcast(FP8X4),
+                rhs_scale=scales[n][:],
+                start=True,
+                stop=True,
+            )
+            nc.scalar.activation(out=gate[n][:, jt, :], in_=bank[:], func=func)
 
         def gather_words():
             nc.vector.tensor_copy(out=xw[:], in_=xw_all[:].indirect(offs_t[:]))
@@ -242,74 +251,74 @@ def tile_picked_ytlstm_cell_p_kernel(
             dst = out[h * HALF : (h + 1) * HALF, u * HALF : (u + 1) * HALF].rearrange("(b i) j -> i b j", b=2)
             nc.sync.dma_start(out=dst, in_=res[:])
 
-        gather_scales()
         gather_words()
-        cast("w2", 0, True)
+        gather_scales()
+        cast("w2", 0, False)
+        cast("w2", 1, True)
         fade_prep(7)
         quantise("w2", 0)
-        cast("w3", 0, True)
-        gate_unit("w2", 0, 0, ACT.Sigmoid, 0)
-        gate_unit("w2", 0, 1, ACT.Sigmoid, 1)
         gather_mem(0)
-        quantise("w3", 0)
-        cast("w2", 1, False)
-        gate_unit("w3", 0, 0, ACT.Tanh, 2)
-        gate_unit("w3", 0, 1, ACT.Tanh, 3)
         quantise("w2", 1)
         gather_mem(1)
-        scale_old(0)
-        gate_unit("w2", 1, 0, ACT.Sigmoid, 0)
-        gate_unit("w2", 1, 1, ACT.Sigmoid, 1)
         gather_mem(2)
+        scale_old(0)
+        gate_row("w2", 0, ACT.Sigmoid, 0)
         scale_old(1)
-        fresh_unit(0, 0)
-        cast("w3", 1, True)
-        gather_mem(3)
-        turn(fresh, 0, 0, True)
+        gate_row("w2", 1, ACT.Sigmoid, 1)
         scale_old(2)
+        cast("w3", 0, False)
+        cast("w3", 1, True)
+        gate_row("w2", 2, ACT.Sigmoid, 2)
+        gate_row("w2", 3, ACT.Sigmoid, 3)
+        quantise("w3", 0)
+        gather_mem(3)
         quantise("w3", 1)
         scale_old(3)
         cast("old", 0, False)
-        gate_unit("w3", 1, 0, ACT.Tanh, 0)
-        gate_unit("w3", 1, 1, ACT.Tanh, 1)
-        turn_ov(0, 2)
-        turn_ov(1, 3)
-        cast("wd", 0, False)
-        quantise("old", 0)
-        cast("wd", 1, True)
-        quantise("wd", 0)
         cast("old", 1, False)
-        turn_ov(2, 6)
-        turn_ov(3, 7)
-        fresh_unit(0, 1)
+        gate_row("w3", 0, ACT.Tanh, 0)
+        gate_row("w3", 1, ACT.Tanh, 1)
+        turn_ov(0, 6)
+        turn_ov(1, 7)
+        quantise("old", 0)
+        cast("wd", 0, False)
+        cast("wd", 1, True)
+        quantise("old", 1)
+        quantise("wd", 0)
+        gate_row("w3", 2, ACT.Tanh, 2)
+        turn_ov(2, 4)
         quantise("wd", 1)
         cast("w1", 0, True)
-        quantise("old", 1)
+        cast("w1", 1, False)
+        gate_row("w3", 3, ACT.Tanh, 3)
+        turn_ov(3, 5)
         short_term(0, 0)
         short_term(1, 1)
-        cast("w1", 1, False)
-        turn(fresh, 0, 1, True)
-        quantise("w1", 0)
-        short_term(2, 0)
-        short_term(3, 1)
-        fresh_unit(1, 0)
         quantise("w1", 1)
+        fresh_unit(0, 0)
+        quantise("w1", 0)
+        short_term(2, 2)
+        short_term(3, 3)
+        fresh_unit(1, 0)
         adjust(0)
         adjust(1)
-        gate_unit("w1", 0, 0, ACT.Sigmoid, 2)
-        gate_unit("w1", 1, 0, ACT.Sigmoid, 3)
-        fresh_unit(1, 1)
+        gate_row("w1", 0, ACT.Sigmoid, 0)
+        gate_row("w1", 1, ACT.Sigmoid, 1)
         adjust(2)
         adjust(3)
-        gate_unit("w1", 0, 1, ACT.Sigmoid, 0)
-        gate_unit("w1", 1, 1, ACT.Sigmoid, 1)
+        gate_row("w1", 2, ACT.Sigmoid, 2)
+        gate_row("w1", 3, ACT.Sigmoid, 3)
+        fresh_unit(0, 1)
+        fresh_unit(1, 1)
         turn(fresh, 1, 0, True)
+        turn(fresh, 1, 1, True)
+        turn(fresh, 0, 0, True)
+        turn(fresh, 0, 1, True)
         kept_unit(0, 0)
         kept_unit(1, 0)
-        turn(fresh, 1, 1, True)
-        kept_unit(0, 1)
         finish(0, 0, True)
-        kept_unit(1, 1)
+        kept_unit(0, 1)
         finish(1, 0, True)
+        kept_unit(1, 1)
         finish(0, 1, False)
         finish(1, 1, True)

@@ -154,6 +154,25 @@ def tile_picked_ytlstm_cell_p_kernel(
             )
             nc.scalar.activation(out=gate[n][:, jt, :], in_=bank[:], func=func)
 
+        last = {}
+
+        def gate_turned(n, func, b):
+            bank = bank_tile(b, [P, 2, HALF])
+            js = slice(HALF, 2 * HALF)
+            for k in range(2):
+                cols = slice((2 + k) * P, (3 + k) * P)
+                nc.tensor.matmul_mx(
+                    out=bank[:, k, :],
+                    lhsT=codes[n][:, cols].bitcast(FP8X4),
+                    lhsT_scale=scales[n][:, cols],
+                    rhs=xw[:, js].bitcast(FP8X4),
+                    rhs_scale=xs[:, js],
+                    start=True,
+                    stop=True,
+                )
+            last[n] = sb("last_" + n, [P, 2, HALF], F32)
+            nc.scalar.activation(out=last[n][:], in_=bank[:], func=func)
+
         def gather_words():
             nc.vector.tensor_copy(out=xw[:], in_=xw_all[:].indirect(offs_t[:]))
 
@@ -251,6 +270,27 @@ def tile_picked_ytlstm_cell_p_kernel(
             dst = out[h * HALF : (h + 1) * HALF, u * HALF : (u + 1) * HALF].rearrange("(b i) j -> i b j", b=2)
             nc.sync.dma_start(out=dst, in_=res[:])
 
+        def turn_last():
+            turned = bank_tile(7, [P, 2, HALF])
+            last["adj"] = turned
+            for b in range(2):
+                for k in range(2):
+                    i0 = HALF + b * P
+                    nc.tensor.transpose(turned[:, b, k * P : (k + 1) * P], adj[:, 2 + k, i0 : i0 + P], ident[:])
+
+        def finish_last():
+            turned = last["adj"]
+            prod = sb("last_prod", [P, 2, HALF], F32)
+            part = sb("last_part", [P, 2, HALF], F32)
+            nc.vector.tensor_tensor(out=prod[:], in0=last["w2"][:], in1=last["w3"][:], op=ALU.mult)
+            nc.vector.tensor_tensor(out=part[:], in0=last["w1"][:], in1=turned[:], op=ALU.mult)
+            dst = out[HALF:, HALF:].rearrange("(b i) j -> i b j", b=2)
+            step = 2
+            for b in range(0, 2, step):
+                res = sb("last_res_%d" % b, [P, step, HALF], F32)
+                nc.vector.tensor_tensor(out=res[:], in0=prod[:, b : b + step, :], in1=part[:, b : b + step, :], op=ALU.add)
+                nc.sync.dma_start(out=dst[:, b : b + step, :], in_=res[:])
+
         gather_words()
         gather_scales()
         cast("w2", 0, False)
@@ -268,8 +308,8 @@ def tile_picked_ytlstm_cell_p_kernel(
         scale_old(2)
         cast("w3", 0, False)
         cast("w3", 1, True)
-        gate_row("w2", 2, ACT.Sigmoid, 2)
-        gate_row("w2", 3, ACT.Sigmoid, 3)
+        gate_unit("w2", 0, 1, ACT.Sigmoid, 2)
+        gate_turned("w2", ACT.Sigmoid, 3)
         quantise("w3", 0)
         gather_mem(3)
         quantise("w3", 1)
@@ -285,12 +325,12 @@ def tile_picked_ytlstm_cell_p_kernel(
         cast("wd", 1, True)
         quantise("old", 1)
         quantise("wd", 0)
-        gate_row("w3", 2, ACT.Tanh, 2)
+        gate_unit("w3", 0, 1, ACT.Tanh, 2)
         turn_ov(2, 4)
         quantise("wd", 1)
         cast("w1", 0, True)
         cast("w1", 1, False)
-        gate_row("w3", 3, ACT.Tanh, 3)
+        gate_turned("w3", ACT.Tanh, 3)
         turn_ov(3, 5)
         short_term(0, 0)
         short_term(1, 1)
@@ -306,12 +346,11 @@ def tile_picked_ytlstm_cell_p_kernel(
         gate_row("w1", 1, ACT.Sigmoid, 1)
         adjust(2)
         adjust(3)
-        gate_row("w1", 2, ACT.Sigmoid, 2)
-        gate_row("w1", 3, ACT.Sigmoid, 3)
+        turn_last()
+        gate_unit("w1", 0, 1, ACT.Sigmoid, 2)
+        gate_turned("w1", ACT.Sigmoid, 3)
         fresh_unit(0, 1)
-        fresh_unit(1, 1)
         turn(fresh, 1, 0, True)
-        turn(fresh, 1, 1, True)
         turn(fresh, 0, 0, True)
         turn(fresh, 0, 1, True)
         kept_unit(0, 0)
@@ -319,6 +358,5 @@ def tile_picked_ytlstm_cell_p_kernel(
         finish(0, 0, True)
         kept_unit(0, 1)
         finish(1, 0, True)
-        kept_unit(1, 1)
-        finish(0, 1, False)
-        finish(1, 1, True)
+        finish(0, 1, True)
+        finish_last()

@@ -33,8 +33,8 @@ def tile_picked_ytlstm_cell_p_kernel(
         def bank_tile(b, shape):
             return psum.tile(shape, F32, name="bank", tag="bank%d" % b)
 
-        def sb(name, shape, dtype):
-            return keep.tile(shape, dtype, name=name, align_bytes=64)
+        def sb(name, shape, dtype, tag=None):
+            return keep.tile(shape, dtype, name=name, tag=tag or name, align_bytes=64)
 
         offs_t = keep.tile([P, PICKED // 16], U16, name="offs_t")
         slot_t = keep.tile([P, PICKED // 16], U16, name="slot_t")
@@ -103,7 +103,7 @@ def tile_picked_ytlstm_cell_p_kernel(
         gate = {n: sb("gate_" + n, [P, 4, UNITS], F32) for n in ("w1", "w2", "w3", "wd")}
         adj = sb("adj", [P, 4, UNITS], F32)
         kept = sb("kept", [P, 4, UNITS], F32)
-        fresh = sb("fresh", [P, 4, UNITS], F32)
+        fresh = {}
 
         def cast(n, h, on_scalar):
             src = (old if n == "old" else w_raw[n])[:, :, h * HALF : (h + 1) * HALF]
@@ -199,9 +199,10 @@ def tile_picked_ytlstm_cell_p_kernel(
             nc.tensor.transpose(fade_bank[:], fade_rows[:], ident[:])
             nc.scalar.activation(out=fm1[:], in_=fade_bank[:, 0:4], func=ACT.Copy, bias=-1.0)
 
-        def fresh_unit(h, u):
+        def fresh_unit(h, u, engine, tag=None):
             w = (slice(None), slice(2 * u, 2 * u + 2), slice(h * HALF, (h + 1) * HALF))
-            nc.vector.tensor_tensor(out=fresh[w], in0=gate["w2"][w], in1=gate["w3"][w], op=ALU.mult)
+            fresh[h, u] = sb("fresh_%d_%d" % (h, u), [P, 2, HALF], F32)[:] if tag is None else tag
+            engine.tensor_tensor(out=fresh[h, u], in0=gate["w2"][w], in1=gate["w3"][w], op=ALU.mult)
 
         def kept_unit(h, u):
             w = (slice(None), slice(2 * u, 2 * u + 2), slice(h * HALF, (h + 1) * HALF))
@@ -252,7 +253,7 @@ def tile_picked_ytlstm_cell_p_kernel(
                     i0 = h * HALF + b * P
                     nc.tensor.matmul(
                         total[:, b, k * P : (k + 1) * P],
-                        src[:, 2 * u + k, i0 : i0 + P],
+                        src[h, u][:, k, b * P : (b + 1) * P] if first else src[:, 2 * u + k, i0 : i0 + P],
                         ident[:],
                         start=(first and b == 0 and k == 0),
                         stop=(not first and b == 1 and k == 1),
@@ -297,19 +298,19 @@ def tile_picked_ytlstm_cell_p_kernel(
         cast("w2", 1, True)
         fade_prep(7)
         quantise("w2", 0)
-        gather_mem(0)
         quantise("w2", 1)
+        gather_mem(0)
         gather_mem(1)
         gather_mem(2)
-        scale_old(0)
         gate_row("w2", 0, ACT.Sigmoid, 0)
-        scale_old(1)
         gate_row("w2", 1, ACT.Sigmoid, 1)
-        scale_old(2)
-        cast("w3", 0, False)
-        cast("w3", 1, True)
         gate_unit("w2", 0, 1, ACT.Sigmoid, 2)
         gate_turned("w2", ACT.Sigmoid, 3)
+        cast("w3", 0, False)
+        cast("w3", 1, True)
+        scale_old(0)
+        scale_old(1)
+        scale_old(2)
         quantise("w3", 0)
         gather_mem(3)
         quantise("w3", 1)
@@ -328,18 +329,19 @@ def tile_picked_ytlstm_cell_p_kernel(
         gate_unit("w3", 0, 1, ACT.Tanh, 2)
         turn_ov(2, 4)
         quantise("wd", 1)
-        cast("w1", 0, True)
         cast("w1", 1, False)
+        cast("w1", 0, False)
         gate_turned("w3", ACT.Tanh, 3)
         turn_ov(3, 5)
         short_term(0, 0)
         short_term(1, 1)
         quantise("w1", 1)
-        fresh_unit(0, 0)
+        fresh_unit(0, 0, nc.vector)
         quantise("w1", 0)
+        pair = sb("fresh_pair", [P, 2, 2, HALF], F32, "grouped_w1_0")
         short_term(2, 2)
         short_term(3, 3)
-        fresh_unit(1, 0)
+        fresh_unit(1, 0, nc.gpsimd, pair[:, 0])
         adjust(0)
         adjust(1)
         gate_row("w1", 0, ACT.Sigmoid, 0)
@@ -349,7 +351,7 @@ def tile_picked_ytlstm_cell_p_kernel(
         turn_last()
         gate_unit("w1", 0, 1, ACT.Sigmoid, 2)
         gate_turned("w1", ACT.Sigmoid, 3)
-        fresh_unit(0, 1)
+        fresh_unit(0, 1, nc.gpsimd, pair[:, 1])
         turn(fresh, 1, 0, True)
         turn(fresh, 0, 0, True)
         turn(fresh, 0, 1, True)

@@ -19,6 +19,7 @@ VISITS = 1024
 PICKED = 512
 UNITS = 512
 HALF = 256
+LAST = 2
 FLOPS = 4 * 2 * 512 * 512 * 512
 
 
@@ -30,11 +31,14 @@ def tile_picked_ytlstm_cell_p_kernel(
         keep = ctx.enter_context(tc.tile_pool(name="keep", bufs=1))
         psum = ctx.enter_context(tc.psum_pool(name="psum", bufs=1))
 
-        def bank_tile(b, shape):
-            return psum.tile(shape, F32, name="bank", tag="bank%d" % b)
-
         def sb(name, shape, dtype, tag=None):
             return keep.tile(shape, dtype, name=name, tag=tag or name, align_bytes=64)
+
+        def bank_tile(b):
+            return psum.tile([P, 4, P], F32, name="bank", tag="bank%d" % b)
+
+        def flat(ap):
+            return ap.rearrange("p a c -> p (a c)")
 
         offs_t = keep.tile([P, PICKED // 16], U16, name="offs_t")
         slot_t = keep.tile([P, PICKED // 16], U16, name="slot_t")
@@ -63,10 +67,15 @@ def tile_picked_ytlstm_cell_p_kernel(
         def load_x():
             nc.sync.dma_start(out=xw_all[:].bitcast(I32), in_=x_words[0].rearrange("p n t -> p (n t)").bitcast(I32))
 
-        def load_xs(q):
-            nc.sync.dma_start(
-                out=xs_all[32 * q : 32 * q + 4, :].bitcast(I32), in_=x_scales[0, 4 * q : 4 * q + 4, :].bitcast(I32)
-            )
+        def load_xs():
+            nc.sync.dma_start(offs_t[:], offs)
+            for q in range(4):
+                nc.sync.dma_start(
+                    out=xs_all[32 * q : 32 * q + 4, :].bitcast(I32), in_=x_scales[0, 4 * q : 4 * q + 4, :].bitcast(I32)
+                )
+
+        def load_slot():
+            nc.sync.dma_start(slot_t[:], slot)
 
         def load_unit():
             nc.sync.dma_start(out=unit_t[:], in_=unit.rearrange("(p t) o -> p (t o)", t=PACK))
@@ -75,103 +84,80 @@ def tile_picked_ytlstm_cell_p_kernel(
             nc.sync.dma_start(out=fade_rows[0:4, :], in_=fade[0:1, :].rearrange("o (c j) -> (o c) j", c=4))
 
         load_x()
-        nc.sync.dma_start(offs_t[:], offs)
-        load_xs(0)
-        load_xs(1)
-        load_xs(2)
-        load_xs(3)
+        load_xs()
         load_w("w2")
-        nc.sync.dma_start(slot_t[:], slot)
+        load_slot()
         load_mem(0)
         load_unit()
         load_fade()
         load_mem(1)
         load_mem(2)
-        load_w("w3")
         load_mem(3)
+        load_w("w3")
         load_w("wd")
         load_w("w1")
 
         xw = sb("xw", [P, PICKED], U32)
         xs = sb("xs", [P, PICKED], U8)
         old = sb("old", [P, PACK, PICKED], F32)
-        ov = sb("ov", [P, PACK, PICKED], F32)
+        ov = {}
         fm1 = sb("fm1", [P, 4], F32)
-        grouped = {}
-        codes = {n: sb("codes_" + n, [P, 512], U32) for n in ("w1", "w2", "w3", "wd", "old")}
-        scales = {n: sb("scales_" + n, [P, 512], U8) for n in ("w1", "w2", "w3", "wd", "old")}
-        gate = {n: sb("gate_" + n, [P, 4, UNITS], F32) for n in ("w1", "w2", "w3", "wd")}
+        names = ("w1", "w2", "w3", "wd", "old")
+        codes = {n: sb("codes_" + n, [P, 512], U32) for n in names}
+        scales = {n: sb("scales_" + n, [P, 512], U8) for n in names}
         adj = sb("adj", [P, 4, UNITS], F32)
-        kept = sb("kept", [P, 4, UNITS], F32)
+        gate = {}
+        grouped = {}
         fresh = {}
+        kept = {}
 
-        def cast(n, h, on_scalar):
-            src = (old if n == "old" else w_raw[n])[:, :, h * HALF : (h + 1) * HALF]
-            dst = sb("grouped_%s_%d" % (n, h), [P, HALF, PACK], BF16)
-            grouped[n, h] = dst
-            o = dst[:].rearrange("p (c i) t -> p c t i", i=4)
+        def cast(n, lo, hi, engine, start=None, width=HALF, tag=None):
+            start = lo if start is None else start
+            if (n, start) not in grouped:
+                grouped[n, start] = sb("grouped_%s_%d" % (n, start), [P, width, PACK], BF16, tag)
+            src = (old if n == "old" else w_raw[n])[:, :, lo:hi]
+            o = grouped[n, start][:, lo - start : hi - start, :].rearrange("p (c i) t -> p c t i", i=4)
             s = src.rearrange("p t (c i) -> p c t i", i=4)
-            if on_scalar:
+            if engine == "S":
                 nc.scalar.copy(out=o, in_=s)
             else:
                 nc.vector.tensor_copy(out=o, in_=s)
 
-        def quantise(n, h):
-            cols = slice(h * HALF, (h + 1) * HALF)
+        def quantise(n, start, width=HALF):
             nc.vector.quantize_mx(
-                out=codes[n][:, cols].bitcast(FP8X4),
-                scales=scales[n][:, cols],
-                in_=grouped[n, h][:].rearrange("p c t -> p (c t)"),
+                out=codes[n][:, start : start + width].bitcast(FP8X4),
+                scales=scales[n][:, start : start + width],
+                in_=grouped[n, start][:].rearrange("p c t -> p (c t)"),
             )
 
-        def gate_unit(n, h, u, func, b):
-            bank = bank_tile(b, [P, 2, HALF])
-            cols = slice(h * HALF, (h + 1) * HALF)
-            for k in range(2):
-                js = slice((2 * u + k) * P, (2 * u + k + 1) * P)
-                nc.tensor.matmul_mx(
-                    out=bank[:, k, :],
-                    lhsT=xw[:, js].bitcast(FP8X4),
-                    lhsT_scale=xs[:, js],
-                    rhs=codes[n][:, cols].bitcast(FP8X4),
-                    rhs_scale=scales[n][:, cols],
-                    start=True,
-                    stop=True,
-                )
-            nc.scalar.activation(out=gate[n][:, 2 * u : 2 * u + 2, cols], in_=bank[:], func=func)
-
-        def gate_row(n, jt, func, b):
-            bank = bank_tile(b, [P, UNITS])
-            js = slice(jt * P, (jt + 1) * P)
+        def mx(dst, still, still_cols, moving, moving_cols):
             nc.tensor.matmul_mx(
-                out=bank[:],
-                lhsT=xw[:, js].bitcast(FP8X4),
-                lhsT_scale=xs[:, js],
-                rhs=codes[n][:].bitcast(FP8X4),
-                rhs_scale=scales[n][:],
+                out=dst,
+                lhsT=still[0][:, still_cols].bitcast(FP8X4),
+                lhsT_scale=still[1][:, still_cols],
+                rhs=moving[0][:, moving_cols].bitcast(FP8X4),
+                rhs_scale=moving[1][:, moving_cols],
                 start=True,
                 stop=True,
             )
-            nc.scalar.activation(out=gate[n][:, jt, :], in_=bank[:], func=func)
 
-        last = {}
+        def block(k):
+            return slice(k * P, (k + 1) * P)
 
-        def gate_turned(n, func, b):
-            bank = bank_tile(b, [P, 2, HALF])
-            js = slice(HALF, 2 * HALF)
-            for k in range(2):
-                cols = slice((2 + k) * P, (3 + k) * P)
-                nc.tensor.matmul_mx(
-                    out=bank[:, k, :],
-                    lhsT=codes[n][:, cols].bitcast(FP8X4),
-                    lhsT_scale=scales[n][:, cols],
-                    rhs=xw[:, js].bitcast(FP8X4),
-                    rhs_scale=xs[:, js],
-                    start=True,
-                    stop=True,
-                )
-            last[n] = sb("last_" + n, [P, 2, HALF], F32)
-            nc.scalar.activation(out=last[n][:], in_=bank[:], func=func)
+        def gate_block(n, i, b, into=None):
+            bank = bank_tile(b)
+            if i >= LAST:
+                mx(flat(bank[:]), (codes[n], scales[n]), block(i), (xw, xs), slice(0, PICKED))
+            else:
+                for jt in range(4):
+                    mx(bank[:, jt, :], (xw, xs), block(jt), (codes[n], scales[n]), block(i))
+            gate[n, i] = sb("gate_%s_%d" % (n, i), [P, 4, P], F32) if into is None else into
+            nc.scalar.activation(out=gate[n, i][:], in_=bank[:], func=ACT.Tanh if n == "w3" else ACT.Sigmoid)
+
+        def short_term(jt, b):
+            bank = bank_tile(b)
+            mx(flat(bank[:]), (codes["old"], scales["old"]), block(jt), (codes["wd"], scales["wd"]), slice(0, UNITS))
+            nc.scalar.activation(out=gate["cs"][:, jt, :], in_=flat(bank[:]), func=ACT.Tanh)
 
         def gather_words():
             nc.vector.tensor_copy(out=xw[:], in_=xw_all[:].indirect(offs_t[:]))
@@ -179,186 +165,150 @@ def tile_picked_ytlstm_cell_p_kernel(
         def gather_scales():
             nc.vector.tensor_copy(out=xs[:], in_=xs_all[:].indirect(offs_t[:]))
 
-        def gather_mem(t):
-            nc.vector.tensor_copy(out=old[:, t, :], in_=mem_t[t][:].indirect(slot_t[:]))
+        def gather_mem(t, lo=0, hi=PICKED):
+            nc.vector.tensor_copy(out=old[:, t, lo:hi], in_=mem_t[t][:].indirect(slot_t[:, lo // 16 : hi // 16]))
 
-        def scale_old(t, engine="S"):
+        def scale_old(t, engine="S", into=None):
+            ov[t] = sb("ov_%d" % t, [P, PICKED], F32)[:] if into is None else into
             if engine == "S":
-                nc.scalar.activation(out=ov[:, t, :], in_=old[:, t, :], func=ACT.Copy, scale=unit_t[:, t : t + 1])
+                nc.scalar.activation(out=ov[t], in_=old[:, t, :], func=ACT.Copy, scale=unit_t[:, t : t + 1])
             elif engine == "V":
-                nc.vector.tensor_scalar(
-                    out=ov[:, t, :], in0=old[:, t, :], scalar1=unit_t[:, t : t + 1], scalar2=None, op0=ALU.mult
-                )
+                nc.vector.tensor_scalar(out=ov[t], in0=old[:, t, :], scalar1=unit_t[:, t : t + 1], scalar2=None, op0=ALU.mult)
             else:
                 nc.gpsimd.tensor_scalar(
-                    out=ov[:, t, :], in0=old[:, t, :], scalar1=unit_t[:, t : t + 1], scalar2=0.0, op0=ALU.mult, op1=ALU.add
+                    out=ov[t], in0=old[:, t, :], scalar1=unit_t[:, t : t + 1], scalar2=0.0, op0=ALU.mult, op1=ALU.add
                 )
 
         def fade_prep(b):
-            fade_bank = bank_tile(b, [P, P])
-            nc.tensor.transpose(fade_bank[:], fade_rows[:], ident[:])
-            nc.scalar.activation(out=fm1[:], in_=fade_bank[:, 0:4], func=ACT.Copy, bias=-1.0)
+            fade_bank = bank_tile(b)
+            nc.tensor.transpose(fade_bank[:, 0, :], fade_rows[:], ident[:])
+            nc.scalar.activation(out=fm1[:], in_=fade_bank[:, 0, 0:4], func=ACT.Copy, bias=-1.0)
 
-        def fresh_unit(h, u, engine, tag=None):
-            w = (slice(None), slice(2 * u, 2 * u + 2), slice(h * HALF, (h + 1) * HALF))
-            fresh[h, u] = sb("fresh_%d_%d" % (h, u), [P, 2, HALF], F32)[:] if tag is None else tag
-            engine.tensor_tensor(out=fresh[h, u], in0=gate["w2"][w], in1=gate["w3"][w], op=ALU.mult)
+        turned = {}
 
-        def kept_unit(h, u):
-            w = (slice(None), slice(2 * u, 2 * u + 2), slice(h * HALF, (h + 1) * HALF))
-            nc.vector.tensor_tensor(out=kept[w], in0=gate["w1"][w], in1=adj[w], op=ALU.mult)
-
-        def short_term(jt, b):
-            js = slice(jt * P, (jt + 1) * P)
-            bank = bank_tile(b, [P, UNITS])
-            nc.tensor.matmul_mx(
-                out=bank[:],
-                lhsT=codes["old"][:, js].bitcast(FP8X4),
-                lhsT_scale=scales["old"][:, js],
-                rhs=codes["wd"][:].bitcast(FP8X4),
-                rhs_scale=scales["wd"][:],
-                start=True,
-                stop=True,
-            )
-            nc.scalar.activation(out=gate["wd"][:, jt, :], in_=bank[:], func=ACT.Tanh)
-
-        turned_ov = {}
-
-        def turn_ov(jt, b):
-            js = slice(jt * P, (jt + 1) * P)
-            turned = bank_tile(b, [P, PACK, P])
-            turned_ov[jt] = turned
-            for t in range(PACK):
-                nc.tensor.transpose(turned[:, t, :], ov[:, t, js], ident[:])
+        def turn_ov(t):
+            for jt in range(4):
+                if t == 0:
+                    turned[jt] = bank_tile(4 + jt)
+                nc.tensor.transpose(turned[jt][:, t, :], ov[t][:, block(jt)], ident[:])
 
         def adjust(jt):
-            turned = turned_ov[jt]
             nc.vector.scalar_tensor_tensor(
                 out=adj[:, jt, :].rearrange("j (p t) -> j p t", t=PACK),
-                in0=gate["wd"][:, jt, :].rearrange("j (p t) -> j p t", t=PACK),
+                in0=gate["cs"][:, jt, :].rearrange("j (p t) -> j p t", t=PACK),
                 scalar=fm1[:, jt : jt + 1],
-                in1=turned[:].rearrange("j t p -> j p t"),
+                in1=turned[jt][:].rearrange("j t p -> j p t"),
                 op0=ALU.mult,
                 op1=ALU.add,
             )
 
+        def fresh_block(i, engine, into=None):
+            fresh[i] = sb("fresh_%d" % i, [P, 4, P], F32)[:] if into is None else into
+            engine.tensor_tensor(out=fresh[i], in0=gate["w2", i][:], in1=gate["w3", i][:], op=ALU.mult)
+
         totals = {}
 
-        def turn(src, h, u, first):
+        def turn(i, src, first, last):
             if first:
-                totals[h, u] = bank_tile(4 + 2 * h + u, [P, 2, HALF])
-            total = totals[h, u]
-            for b in range(2):
-                for k in range(2):
-                    i0 = h * HALF + b * P
-                    nc.tensor.matmul(
-                        total[:, b, k * P : (k + 1) * P],
-                        src[h, u][:, k, b * P : (b + 1) * P] if first else src[:, 2 * u + k, i0 : i0 + P],
-                        ident[:],
-                        start=(first and b == 0 and k == 0),
-                        stop=(not first and b == 1 and k == 1),
-                        is_transpose=True,
-                    )
+                totals[i] = bank_tile(4 + i)
+            for jt in range(4):
+                nc.tensor.matmul(
+                    totals[i][:, jt, :], src[:, jt, :], ident[:], start=first and jt == 0, stop=last and jt == 3, is_transpose=True
+                )
 
-        def finish(h, u, on_scalar):
-            turn(kept, h, u, False)
-            total = totals[h, u]
-            res = sb("res_%d_%d" % (h, u), [P, 2, HALF], F32)
-            if on_scalar:
-                nc.scalar.copy(out=res[:], in_=total[:])
+        def kept_block(i):
+            kept[i] = sb("kept_%d" % i, [P, 4, P], F32)
+            nc.vector.tensor_tensor(out=kept[i][:], in0=gate["w1", i][:], in1=adj[:, :, block(i)], op=ALU.mult)
+
+        def finish(i, engine):
+            res = sb("res_%d" % i, [P, 4, P], F32)
+            if engine == "S":
+                nc.scalar.copy(out=res[:], in_=totals[i][:])
             else:
-                nc.vector.tensor_copy(out=res[:], in_=total[:])
-            dst = out[h * HALF : (h + 1) * HALF, u * HALF : (u + 1) * HALF].rearrange("(b i) j -> i b j", b=2)
-            nc.sync.dma_start(out=dst, in_=res[:])
+                nc.vector.tensor_copy(out=res[:], in_=totals[i][:])
+            nc.sync.dma_start(out=out[block(i), :], in_=flat(res[:]))
 
-        def turn_last():
-            turned = bank_tile(7, [P, 2, HALF])
-            last["adj"] = turned
-            for b in range(2):
-                for k in range(2):
-                    i0 = HALF + b * P
-                    nc.tensor.transpose(turned[:, b, k * P : (k + 1) * P], adj[:, 2 + k, i0 : i0 + P], ident[:])
+        part = {}
 
-        def finish_last():
-            turned = last["adj"]
-            prod = sb("last_prod", [P, 2, HALF], F32)
-            part = sb("last_part", [P, 2, HALF], F32)
-            nc.vector.tensor_tensor(out=prod[:], in0=last["w2"][:], in1=last["w3"][:], op=ALU.mult)
-            nc.vector.tensor_tensor(out=part[:], in0=last["w1"][:], in1=turned[:], op=ALU.mult)
-            dst = out[HALF:, HALF:].rearrange("(b i) j -> i b j", b=2)
-            step = 2
-            for b in range(0, 2, step):
-                res = sb("last_res_%d" % b, [P, step, HALF], F32)
-                nc.vector.tensor_tensor(out=res[:], in0=prod[:, b : b + step, :], in1=part[:, b : b + step, :], op=ALU.add)
-                nc.sync.dma_start(out=dst[:, b : b + step, :], in_=res[:])
+        def part_block(i):
+            part[i] = sb("part_%d" % i, [P, 4, P], F32)
+            nc.vector.tensor_tensor(out=part[i][:], in0=gate["w1", i][:], in1=totals[i][:], op=ALU.mult)
+
+        def finish_turned(i, pieces):
+            for lo, hi in pieces:
+                res = sb("res_%d_%d" % (i, lo), [P, hi - lo, P], F32)
+                nc.vector.tensor_tensor(out=res[:], in0=part[i][:, lo:hi], in1=fresh[i][:, lo:hi], op=ALU.add)
+                nc.sync.dma_start(out=out[block(i), lo * P : hi * P], in_=flat(res[:]))
 
         gather_words()
         gather_scales()
-        cast("w2", 0, False)
-        cast("w2", 1, True)
+        cast("w2", 0, 256, "V")
+        cast("w2", 256, 512, "S")
         fade_prep(7)
         quantise("w2", 0)
-        quantise("w2", 1)
+        quantise("w2", 256)
         gather_mem(0)
         gather_mem(1)
-        gather_mem(2)
-        gate_row("w2", 0, ACT.Sigmoid, 0)
-        gate_row("w2", 1, ACT.Sigmoid, 1)
-        gate_unit("w2", 0, 1, ACT.Sigmoid, 2)
-        gate_turned("w2", ACT.Sigmoid, 3)
-        cast("w3", 0, False)
-        cast("w3", 1, True)
+        for lo in (0, HALF):
+            gather_mem(2, lo, lo + HALF)
+            gather_mem(3, lo, lo + HALF)
+        for i in range(4):
+            gate_block("w2", i, i)
         scale_old(0)
         scale_old(1)
+        cast("old", 0, 256, "S")
         scale_old(2)
-        quantise("w3", 0)
-        gather_mem(3)
-        quantise("w3", 1)
-        scale_old(3)
-        cast("old", 0, False)
-        cast("old", 1, False)
-        gate_row("w3", 0, ACT.Tanh, 0)
-        gate_row("w3", 1, ACT.Tanh, 1)
-        turn_ov(0, 6)
-        turn_ov(1, 7)
+        for t in range(3):
+            turn_ov(t)
+        cast("old", 256, 512, "V")
         quantise("old", 0)
-        cast("wd", 0, False)
-        cast("wd", 1, True)
-        quantise("old", 1)
+        quantise("old", 256)
+        cast("w3", 128, 256, "S", 0)
+        cast("w3", 256, 512, "S")
+        cast("w3", 0, 128, "V")
+        quantise("w3", 0)
+        quantise("w3", 256)
+        cast("wd", 0, 256, "V")
+        cast("wd", 256, 512, "S")
         quantise("wd", 0)
-        gate_unit("w3", 0, 1, ACT.Tanh, 2)
-        turn_ov(2, 4)
-        quantise("wd", 1)
-        cast("w1", 1, False)
-        cast("w1", 0, False)
-        gate_turned("w3", ACT.Tanh, 3)
-        turn_ov(3, 5)
-        short_term(0, 0)
-        short_term(1, 1)
-        quantise("w1", 1)
-        fresh_unit(0, 0, nc.vector)
+        quantise("wd", 256)
+        late_g = sb("late_g", [P, 4, 4, P], F32, "raw_wd")
+        scale_old(3, "V")
+        turn_ov(3)
+        gate["cs"] = sb("cs", [P, 4, UNITS], F32)
+        gate_block("w3", 0, 0, late_g[:, 0])
+        gate_block("w3", 1, 1, late_g[:, 1])
+        cast("w1", 0, 256, "V")
+        cast("w1", 256, 512, "V")
+        short_term(0, 2)
+        short_term(1, 3)
+        gate_block("w3", 2, 0, late_g[:, 2])
         quantise("w1", 0)
-        pair = sb("fresh_pair", [P, 2, 2, HALF], F32, "grouped_w1_0")
-        short_term(2, 2)
-        short_term(3, 3)
-        fresh_unit(1, 0, nc.gpsimd, pair[:, 0])
-        adjust(0)
-        adjust(1)
-        gate_row("w1", 0, ACT.Sigmoid, 0)
-        gate_row("w1", 1, ACT.Sigmoid, 1)
-        adjust(2)
-        adjust(3)
-        turn_last()
-        gate_unit("w1", 0, 1, ACT.Sigmoid, 2)
-        gate_turned("w1", ACT.Sigmoid, 3)
-        fresh_unit(0, 1, nc.gpsimd, pair[:, 1])
-        turn(fresh, 1, 0, True)
-        turn(fresh, 0, 0, True)
-        turn(fresh, 0, 1, True)
-        kept_unit(0, 0)
-        kept_unit(1, 0)
-        finish(0, 0, True)
-        kept_unit(0, 1)
-        finish(1, 0, True)
-        finish(0, 1, True)
-        finish_last()
+        fresh_block(0, nc.vector, sb("fresh_first", [P, 4, P], F32, "grouped_wd_256")[:])
+        quantise("w1", 256)
+        pair = sb("fresh_pair", [P, 2, 4, P], F32, "grouped_w1_0")
+        short_term(2, 1)
+        short_term(3, 2)
+        fresh_block(1, nc.gpsimd, pair[:, 0])
+        fresh_block(2, nc.gpsimd, pair[:, 1])
+        for jt in range(4):
+            adjust(jt)
+        gate_block("w1", 0, 3)
+        gate_block("w1", 1, 0)
+        gate_block("w1", 2, 1)
+        gate_block("w3", 3, 2, late_g[:, 3])
+        gate_block("w1", 3, 3)
+        turn(0, fresh[0], True, False)
+        turn(2, adj[:, :, block(2)], True, True)
+        turn(3, adj[:, :, block(3)], True, True)
+        turn(1, fresh[1], True, False)
+        for i in range(LAST):
+            kept_block(i)
+            if i == 0:
+                fresh_block(3, nc.gpsimd, sb("fresh_last", [P, 4, P], F32, "gate_w1_0")[:])
+            turn(i, kept[i], False, True)
+            finish(i, "S")
+        part_block(2)
+        part_block(3)
+        finish_turned(2, [(0, 4)])
+        finish_turned(3, [(0, 2), (2, 4)])

@@ -123,11 +123,12 @@ def tile_picked_ytlstm_cell_p_kernel(
             else:
                 nc.vector.tensor_copy(out=o, in_=s)
 
-        def quantise(n, start, width=HALF):
+        def quantise(n, start, width=HALF, base=None):
+            base = start if base is None else base
             nc.vector.quantize_mx(
                 out=codes[n][:, start : start + width].bitcast(FP8X4),
                 scales=scales[n][:, start : start + width],
-                in_=grouped[n, start][:].rearrange("p c t -> p (c t)"),
+                in_=grouped[n, base][:, start - base : start - base + width, :].rearrange("p c t -> p (c t)"),
             )
 
         def mx(dst, still, still_cols, moving, moving_cols):
@@ -278,26 +279,24 @@ def tile_picked_ytlstm_cell_p_kernel(
         gate["cs"] = sb("cs", [P, 4, UNITS], F32)
         gate_block("w3", 0, 0, late_g[:, 0])
         gate_block("w3", 1, 1, late_g[:, 1])
+        gate_block("w3", 2, 2, late_g[:, 2])
         cast("w1", 0, 256, "V")
         cast("w1", 256, 512, "V")
-        short_term(0, 2)
-        short_term(1, 3)
-        gate_block("w3", 2, 0, late_g[:, 2])
+        short_term(0, 3)
+        short_term(1, 0)
         quantise("w1", 0)
-        fresh_block(0, nc.vector, sb("fresh_first", [P, 4, P], F32, "grouped_wd_256")[:])
         quantise("w1", 256)
         pair = sb("fresh_pair", [P, 2, 4, P], F32, "grouped_w1_0")
         short_term(2, 1)
         short_term(3, 2)
-        fresh_block(1, nc.gpsimd, pair[:, 0])
-        fresh_block(2, nc.gpsimd, pair[:, 1])
+        fresh_block(0, nc.gpsimd, pair[:, 0])
+        fresh_block(1, nc.gpsimd, pair[:, 1])
         for jt in range(4):
             adjust(jt)
         gate_block("w1", 0, 3)
         gate_block("w1", 1, 0)
         gate_block("w1", 2, 1)
-        gate_block("w3", 3, 2, late_g[:, 3])
-        gate_block("w1", 3, 3)
+        gate_block("w1", 3, 2)
         turn(0, fresh[0], True, False)
         turn(2, adj[:, :, block(2)], True, True)
         turn(3, adj[:, :, block(3)], True, True)
@@ -305,10 +304,15 @@ def tile_picked_ytlstm_cell_p_kernel(
         for i in range(LAST):
             kept_block(i)
             if i == 0:
-                fresh_block(3, nc.gpsimd, sb("fresh_last", [P, 4, P], F32, "gate_w1_0")[:])
+                fresh_block(2, nc.gpsimd, sb("fresh_third", [P, 4, P], F32, "gate_w1_0")[:])
             turn(i, kept[i], False, True)
             finish(i, "S")
+            if i == 0:
+                gate_block("w3", 3, 3, late_g[:, 3])
         part_block(2)
         part_block(3)
         finish_turned(2, [(0, 4)])
+        fresh[3] = sb("fresh_3", [P, 4, P], F32)[:]
+        for lo in (0, 2):
+            nc.vector.tensor_tensor(out=fresh[3][:, lo : lo + 2], in0=gate["w2", 3][:, lo : lo + 2], in1=gate["w3", 3][:, lo : lo + 2], op=ALU.mult)
         finish_turned(3, [(0, 2), (2, 4)])

@@ -191,14 +191,14 @@ def tile_picked_ytlstm_cell_p_kernel(
             for jt in range(4):
                 if t == 0:
                     turned[jt] = bank_tile(4 + jt)
-                nc.tensor.transpose(turned[jt][:, t, :], ov[t][:, block(jt)], ident[:])
+                nc.tensor.transpose(flat(turned[jt][:]).rearrange("j (p t) -> j t p", t=PACK)[:, t, :], ov[t][:, block(jt)], ident[:])
 
         def adjust(jt):
             nc.vector.scalar_tensor_tensor(
-                out=adj[:, jt, :].rearrange("j (p t) -> j p t", t=PACK),
-                in0=gate["cs"][:, jt, :].rearrange("j (p t) -> j p t", t=PACK),
+                out=adj[:, jt, :],
+                in0=gate["cs"][:, jt, :],
                 scalar=fm1[:, jt : jt + 1],
-                in1=turned[jt][:].rearrange("j t p -> j p t"),
+                in1=flat(turned[jt][:]),
                 op0=ALU.mult,
                 op1=ALU.add,
             )

from contextlib import ExitStack

import concourse.mybir as mybir
from concourse.masks import make_identity

F32 = mybir.dt.float32
BF16 = mybir.dt.bfloat16
I32 = mybir.dt.int32
U32 = mybir.dt.uint32
U16 = mybir.dt.uint16
U8 = mybir.dt.uint8
FP8X4 = mybir.dt.float8_e4m3fn_x4
ACT = mybir.ActivationFunctionType
ALU = mybir.AluOpType

P = 128
PACK = 4
VISITS = 1024
PICKED = 512
UNITS = 512
HALF = 256
LAST = 2
FLOPS = 4 * 2 * 512 * 512 * 512


def tile_picked_ytlstm_cell_p_kernel(
    tc, x_words, x_scales, mem, wd, w1, w2, w3, unit, fade, offs, slot, out
):
    nc = tc.nc
    with ExitStack() as ctx:
        keep = ctx.enter_context(tc.tile_pool(name="keep", bufs=1))
        psum = ctx.enter_context(tc.psum_pool(name="psum", bufs=1))

        def sb(name, shape, dtype, tag=None):
            return keep.tile(shape, dtype, name=name, tag=tag or name, align_bytes=64)

        def bank_tile(b):
            return psum.tile([P, 4, P], F32, name="bank", tag="bank%d" % b)

        def flat(ap):
            return ap.rearrange("p a c -> p (a c)")

        offs_t = keep.tile([P, PICKED // 16], U16, name="offs_t")
        slot_t = keep.tile([P, PICKED // 16], U16, name="slot_t")
        xw_all = sb("xw_all", [P, VISITS], U32)
        xs_all = sb("xs_all", [P, VISITS], U8)
        fade_rows = sb("fade_rows", [P, P], F32)
        ident = sb("ident", [P, P], F32)
        unit_t = sb("unit_t", [P, PACK], F32)
        mem_t = [sb("mem_%d" % t, [P, VISITS], F32) for t in range(PACK)]
        weights = {"w1": w1, "w2": w2, "w3": w3, "wd": wd}
        w_raw = {n: sb("raw_" + n, [P, PACK, UNITS], F32) for n in weights}

        nc.gpsimd.memset(xs_all[:].bitcast(I32), 0)
        warm = sb("warm", [P, 2], F32)
        nc.gpsimd.memset(warm[:, 0:1], 0.0)
        nc.scalar.activation(out=warm[:, 1:2], in_=warm[:, 0:1], func=ACT.Sigmoid)
        nc.gpsimd.memset(fade_rows[:], 0.0)
        make_identity(nc, ident[:])

        def load_w(n):
            nc.sync.dma_start(out=w_raw[n][:], in_=weights[n].rearrange("(p t) n -> p t n", t=PACK))

        def load_mem(t):
            nc.sync.dma_start(out=mem_t[t][:], in_=mem.rearrange("(p t) c -> t p c", t=PACK)[t])

        def load_x():
            nc.sync.dma_start(out=xw_all[:].bitcast(I32), in_=x_words[0].rearrange("p n t -> p (n t)").bitcast(I32))

        def load_xs():
            nc.sync.dma_start(offs_t[:], offs)
            for q in range(4):
                nc.sync.dma_start(
                    out=xs_all[32 * q : 32 * q + 4, :].bitcast(I32), in_=x_scales[0, 4 * q : 4 * q + 4, :].bitcast(I32)
                )

        def load_slot():
            nc.sync.dma_start(slot_t[:], slot)

        def load_unit():
            nc.sync.dma_start(out=unit_t[:], in_=unit.rearrange("(p t) o -> p (t o)", t=PACK))

        def load_fade():
            nc.sync.dma_start(out=fade_rows[0:4, :], in_=fade[0:1, :].rearrange("o (c j) -> (o c) j", c=4))

        load_x()
        load_xs()
        load_w("w2")
        load_slot()
        load_mem(0)
        load_unit()
        load_fade()
        load_mem(1)
        load_mem(2)
        load_mem(3)
        load_w("w3")
        load_w("wd")
        load_w("w1")

        xw = sb("xw", [P, PICKED], U32)
        xs = sb("xs", [P, PICKED], U8)
        old = sb("old", [P, PACK, PICKED], F32)
        ov = {}
        fm1 = sb("fm1", [P, 4], F32)
        names = ("w1", "w2", "w3", "wd", "old")
        codes = {n: sb("codes_" + n, [P, 512], U32) for n in names}
        scales = {n: sb("scales_" + n, [P, 512], U8) for n in names}
        adj = sb("adj", [P, 4, UNITS], F32)
        gate = {}
        grouped = {}
        fresh = {}
        kept = {}

        def cast(n, lo, hi, engine, start=None, width=HALF, tag=None):
            start = lo if start is None else start
            if (n, start) not in grouped:
                grouped[n, start] = sb("grouped_%s_%d" % (n, start), [P, width, PACK], BF16, tag)
            src = (old if n == "old" else w_raw[n])[:, :, lo:hi]
            o = grouped[n, start][:, lo - start : hi - start, :].rearrange("p (c i) t -> p c t i", i=4)
            s = src.rearrange("p t (c i) -> p c t i", i=4)
            if engine == "S":
                nc.scalar.copy(out=o, in_=s)
            else:
                nc.vector.tensor_copy(out=o, in_=s)

        def quantise(n, start, width=HALF, base=None):
            base = start if base is None else base
            nc.vector.quantize_mx(
                out=codes[n][:, start : start + width].bitcast(FP8X4),
                scales=scales[n][:, start : start + width],
                in_=grouped[n, base][:, start - base : start - base + width, :].rearrange("p c t -> p (c t)"),
            )

        def mx(dst, still, still_cols, moving, moving_cols):
            nc.tensor.matmul_mx(
                out=dst,
                lhsT=still[0][:, still_cols].bitcast(FP8X4),
                lhsT_scale=still[1][:, still_cols],
                rhs=moving[0][:, moving_cols].bitcast(FP8X4),
                rhs_scale=moving[1][:, moving_cols],
                start=True,
                stop=True,
            )

        def block(k):
            return slice(k * P, (k + 1) * P)

        def gate_block(n, i, b, into=None):
            bank = bank_tile(b)
            if i >= LAST:
                mx(flat(bank[:]), (codes[n], scales[n]), block(i), (xw, xs), slice(0, PICKED))
            else:
                for jt in range(4):
                    mx(bank[:, jt, :], (xw, xs), block(jt), (codes[n], scales[n]), block(i))
            gate[n, i] = sb("gate_%s_%d" % (n, i), [P, 4, P], F32) if into is None else into
            nc.scalar.activation(out=gate[n, i][:], in_=bank[:], func=ACT.Tanh if n == "w3" else ACT.Sigmoid)

        def short_term(jt, b):
            bank = bank_tile(b)
            mx(flat(bank[:]), (codes["old"], scales["old"]), block(jt), (codes["wd"], scales["wd"]), slice(0, UNITS))
            nc.scalar.activation(out=gate["cs"][:, jt, :], in_=flat(bank[:]), func=ACT.Tanh)

        def gather_words():
            nc.vector.tensor_copy(out=xw[:], in_=xw_all[:].indirect(offs_t[:]))

        def gather_scales():
            nc.vector.tensor_copy(out=xs[:], in_=xs_all[:].indirect(offs_t[:]))

        def gather_mem(t, lo=0, hi=PICKED):
            nc.vector.tensor_copy(out=old[:, t, lo:hi], in_=mem_t[t][:].indirect(slot_t[:, lo // 16 : hi // 16]))

        def scale_old(t, engine="S", into=None):
            ov[t] = sb("ov_%d" % t, [P, PICKED], F32)[:] if into is None else into
            if engine == "S":
                nc.scalar.activation(out=ov[t], in_=old[:, t, :], func=ACT.Copy, scale=unit_t[:, t : t + 1])
            elif engine == "V":
                nc.vector.tensor_scalar(out=ov[t], in0=old[:, t, :], scalar1=unit_t[:, t : t + 1], scalar2=None, op0=ALU.mult)
            else:
                nc.gpsimd.tensor_scalar(
                    out=ov[t], in0=old[:, t, :], scalar1=unit_t[:, t : t + 1], scalar2=0.0, op0=ALU.mult, op1=ALU.add
                )

        def fade_prep(b):
            fade_bank = bank_tile(b)
            nc.tensor.transpose(fade_bank[:, 0, :], fade_rows[:], ident[:])
            nc.scalar.activation(out=fm1[:], in_=fade_bank[:, 0, 0:4], func=ACT.Copy, bias=-1.0)

        turned = {}

        def turn_ov(t):
            for jt in range(4):
                if t == 0:
                    turned[jt] = bank_tile(4 + jt)
                nc.tensor.transpose(flat(turned[jt][:]).rearrange("j (p t) -> j t p", t=PACK)[:, t, :], ov[t][:, block(jt)], ident[:])

        def adjust(jt):
            nc.vector.scalar_tensor_tensor(
                out=adj[:, jt, :],
                in0=gate["cs"][:, jt, :],
                scalar=fm1[:, jt : jt + 1],
                in1=flat(turned[jt][:]),
                op0=ALU.mult,
                op1=ALU.add,
            )

        def fresh_block(i, engine, into=None):
            fresh[i] = sb("fresh_%d" % i, [P, 4, P], F32)[:] if into is None else into
            engine.tensor_tensor(out=fresh[i], in0=gate["w2", i][:], in1=gate["w3", i][:], op=ALU.mult)

        totals = {}

        def turn(i, src, first, last):
            if first:
                totals[i] = bank_tile(4 + i)
            for jt in range(4):
                nc.tensor.matmul(
                    totals[i][:, jt, :], src[:, jt, :], ident[:], start=first and jt == 0, stop=last and jt == 3, is_transpose=True
                )

        def kept_block(i):
            kept[i] = sb("kept_%d" % i, [P, 4, P], F32)
            nc.vector.tensor_tensor(out=kept[i][:], in0=gate["w1", i][:], in1=adj[:, :, block(i)], op=ALU.mult)

        def finish(i, engine):
            res = sb("res_%d" % i, [P, 4, P], F32)
            if engine == "S":
                nc.scalar.copy(out=res[:], in_=totals[i][:])
            else:
                nc.vector.tensor_copy(out=res[:], in_=totals[i][:])
            nc.sync.dma_start(out=out[block(i), :], in_=flat(res[:]))

        part = {}

        def part_block(i):
            part[i] = sb("part_%d" % i, [P, 4, P], F32)
            nc.vector.tensor_tensor(out=part[i][:], in0=gate["w1", i][:], in1=totals[i][:], op=ALU.mult)

        def finish_turned(i, pieces):
            for lo, hi in pieces:
                res = sb("res_%d_%d" % (i, lo), [P, hi - lo, P], F32)
                nc.vector.tensor_tensor(out=res[:], in0=part[i][:, lo:hi], in1=fresh[i][:, lo:hi], op=ALU.add)
                nc.sync.dma_start(out=out[block(i), lo * P : hi * P], in_=flat(res[:]))

        gather_words()
        gather_scales()
        cast("w2", 0, 256, "V")
        cast("w2", 256, 512, "S")
        fade_prep(7)
        quantise("w2", 0)
        quantise("w2", 256)
        gather_mem(0)
        gather_mem(1)
        for lo in (0, HALF):
            gather_mem(2, lo, lo + HALF)
            gather_mem(3, lo, lo + HALF)
        for i in range(4):
            gate_block("w2", i, i)
        scale_old(0)
        scale_old(1)
        cast("old", 0, 256, "S")
        scale_old(2)
        for t in range(3):
            turn_ov(t)
        cast("old", 256, 512, "V")
        quantise("old", 0)
        quantise("old", 256)
        cast("w3", 128, 256, "S", 0)
        cast("w3", 256, 512, "S")
        cast("w3", 0, 128, "V")
        quantise("w3", 0)
        quantise("w3", 256)
        cast("wd", 0, 256, "V")
        cast("wd", 256, 512, "S")
        quantise("wd", 0)
        quantise("wd", 256)
        late_g = sb("late_g", [P, 4, 4, P], F32, "raw_wd")
        scale_old(3, "V")
        turn_ov(3)
        gate["cs"] = sb("cs", [P, 4, UNITS], F32)
        gate_block("w3", 0, 0, late_g[:, 0])
        gate_block("w3", 1, 1, late_g[:, 1])
        gate_block("w3", 2, 2, late_g[:, 2])
        cast("w1", 0, 256, "V")
        cast("w1", 256, 512, "V")
        short_term(0, 3)
        short_term(1, 0)
        quantise("w1", 0)
        quantise("w1", 256)
        pair = sb("fresh_pair", [P, 2, 4, P], F32, "grouped_w1_0")
        short_term(2, 1)
        short_term(3, 2)
        fresh_block(0, nc.gpsimd, pair[:, 0])
        fresh_block(1, nc.gpsimd, pair[:, 1])
        for jt in range(4):
            adjust(jt)
        gate_block("w1", 0, 3)
        gate_block("w1", 1, 0)
        gate_block("w1", 2, 1)
        gate_block("w1", 3, 2)
        turn(0, fresh[0], True, False)
        turn(2, adj[:, :, block(2)], True, True)
        turn(3, adj[:, :, block(3)], True, True)
        turn(1, fresh[1], True, False)
        for i in range(LAST):
            kept_block(i)
            if i == 0:
                fresh_block(2, nc.gpsimd, sb("fresh_third", [P, 4, P], F32, "gate_w1_0")[:])
            turn(i, kept[i], False, True)
            finish(i, "S")
            if i == 0:
                gate_block("w3", 3, 3, late_g[:, 3])
        part_block(2)
        part_block(3)
        finish_turned(2, [(0, 4)])
        fresh[3] = sb("fresh_3", [P, 4, P], F32)[:]
        for lo in (0, 2):
            nc.vector.tensor_tensor(out=fresh[3][:, lo : lo + 2], in0=gate["w2", 3][:, lo : lo + 2], in1=gate["w3", 3][:, lo : lo + 2], op=ALU.mult)
        finish_turned(3, [(0, 2), (2, 4)])
